import numpy as np, ml_dtypes
CORES = [3,7,11,15,131,135,139,143]
N = 8
import mx_ref
BF = ml_dtypes.bfloat16
def entries(a):
    return np.ascontiguousarray(a.T).reshape(-1)
def table(e):
    return np.ascontiguousarray(np.reshape(e, (-1, 16)).T).astype(np.int32)
def cols(t, e):
    v = np.concatenate([t.reshape(128, -1, 4), np.zeros((128, 1, 4), BF)], axis=1)
    return np.ascontiguousarray(v[:, e]).reshape(128, -1)
def f(rng, *shape):
    return mx_ref.flush((rng.standard_normal(shape, dtype=np.float32) * np.exp2(rng.integers(-2, 3, shape[:-1] + (1,)))).astype(BF))
def wide(rng, *shape, cols=0):
    v = rng.standard_normal(shape, dtype=np.float32) * np.exp2(rng.integers(-12, 13, shape)).astype(np.float32)
    if cols: v *= np.repeat(np.exp2(rng.integers(-cols, cols + 1, shape[:-2] + (1, shape[-1] // 4))) * (rng.random(shape[:-2] + (1, shape[-1] // 4)) > 0.0625), 4, axis=-1).astype(np.float32)
    return mx_ref.flush(v.astype(BF))
TA, TB, CI, CJ, JW = 256, 256, 24, 64, 384
SIDE = [0 if c < 128 else 1 for c in CORES]
GCOL = [SIDE[:r].count(SIDE[r]) for r in range(N)]
def fill(rng, total, cap, wd, first, back):
    n = np.zeros(N, int)
    for q in first: n[q] = min(cap, total - n.sum())
    while n.sum() < total:
        q = rng.integers(0, N)
        if n[q] < cap: n[q] += 1
    s, used = np.full((N, cap), -1), []
    for q in range(N):
        k, v = rng.permutation(cap)[:n[q]], rng.integers(0, wd, n[q])
        if back: k, v = np.sort(k), np.sort(v)[::-1]
        s[q, k] = v; used += list(q * cap + k)
    return s, (np.sort(used)[::-1] if back else rng.permutation(used))
def lists(rng, full=False, own=False, back=False, alike=False):
    A, B = [], []
    for i in range(2):
        A.append(fill(rng, 128, CI, TA, rng.permutation(N) if full else [r for r in range(N) if own and SIDE[r] == i], back))
    for k in range(4):
        B.append(fill(rng, JW, CJ, TB, rng.permutation(N) if full else [r for r in range(N) if own and GCOL[r] == k], back))
    if alike: B = [B[0]] * 4
    return {"sa": np.stack([table(np.concatenate([A[i][0][q] for i in range(2)])) for q in range(N)]),
            "sb": np.stack([table(np.concatenate([B[k][0][q] for k in range(4)])) for q in range(N)]),
            "pi": np.stack([table(A[SIDE[r]][1]) for r in range(N)]), "pj": np.stack([table(B[GCOL[r]][1]) for r in range(N)])}
def setup_inputs(rng):
    return {"a": f(rng, N, 128, 4 * TA), "b": f(rng, N, 128, 4 * TB), **lists(rng)}
def setup_inputs_alike(rng):
    return {**setup_inputs(rng), **lists(rng, alike=True)}
def setup_inputs_full(rng):
    return {**setup_inputs(rng), **lists(rng, full=True)}
def setup_inputs_own(rng):
    return {**setup_inputs(rng), **lists(rng, own=True)}
def setup_inputs_reversed(rng):
    return {**setup_inputs(rng), **lists(rng, back=True)}
def setup_inputs_spread(rng):
    d = setup_inputs(rng); d["a"], d["b"] = wide(rng, N, 128, 4 * TA, cols=6), wide(rng, N, 128, 4 * TB, cols=6); return d
def check_inputs(d):
    bad = []
    for s, p, wd, cap, total, place in (("sa", "pi", TA, CI, 128, SIDE), ("sb", "pj", TB, CJ, JW, GCOL)):
        e = np.stack([entries(d[s][q]) for q in range(N)])
        if e.min() < -1 or e.max() >= wd: bad.append(s)
        for r in range(N):
            v = e[:, cap * place[r]:cap * place[r] + cap].reshape(-1)
            if (v >= 0).sum() != total: bad.append(s + " count")
            t = entries(d[p][r])
            if t.min() < 0 or t.max() >= N * cap: bad.append(p); continue
            if len(set(t.tolist())) != total or (v[t] < 0).any(): bad.append(p + " slots")
            if (d[p][r] != d[p][place.index(place[r])]).any(): bad.append(p + " not the same")
    return bad
def reference(a, b, sa, sb, pi, pj):
    y = np.zeros((N, 128, JW), np.float32)
    for r in range(N):
        i, k = SIDE[r], GCOL[r]
        A = np.concatenate([cols(a[q], entries(sa[q])[CI * i:CI * i + CI]) for q in range(N)], axis=1)
        B = np.concatenate([cols(b[q], entries(sb[q])[CJ * k:CJ * k + CJ]) for q in range(N)], axis=1)
        y[r] = mx_ref.matmul(mx_ref.quantize(cols(A, entries(pi[r]))), mx_ref.quantize(cols(B, entries(pj[r]))))
    return {"y": y}

@@ -1,0 +1,268 @@
+from concourse.bass import DstId, RemoteDMATransfer, IndirectOffsetOnAxis
+from concourse.mybir import dt, AluOpType, AxisListType, ActivationFunctionType
+
+N, CI, CJ, JW = 8, 24, 64, 384
+CODES = "float8_e4m3fn_x4"
+RELAY, NEIGH, DIRECT, OWN, AEND = 0, 72, 96, 168, 200
+SET1 = 72
+MISS = 1000
+
+SCRATCH = {
+    "aw": ("sbuf", [128, 1032], "bfloat16"), "bw": ("sbuf", [128, 1032], "bfloat16"),
+    "ha": ("sbuf", [128, 512], "bfloat16"), "hb": ("sbuf", [128, 1024], "bfloat16"),
+    "qa": ("sbuf", [128, 128], CODES), "za": ("sbuf", [128, 128], "uint8"),
+    "qb": ("sbuf", [128, 256], CODES), "zb": ("sbuf", [128, 256], "uint8"),
+    "ac": ("sbuf", [128, AEND], CODES), "az": ("sbuf", [128, AEND], "uint8"),
+    "bc": ("sbuf", [128, 512], CODES), "bz": ("sbuf", [128, 512], "uint8"),
+    "la": ("sbuf", [128, 3], "int32"), "lb": ("sbuf", [128, 16], "int32"),
+    "lp": ("sbuf", [128, 8], "int32"), "lj": ("sbuf", [128, 24], "int32"),
+    "oa": ("sbuf", [128, 16], "uint16"), "ob": ("sbuf", [128, 64], "uint16"),
+    "opi": ("sbuf", [128, 8], "uint16"), "opj": ("sbuf", [128, 24], "uint16"),
+    "ip": ("sbuf", [128, 1], "int32"), "ix": ("sbuf", [128, 1], "int32"),
+    "cc": ("sbuf", [128, AEND], "float32"),
+    "pf": ("sbuf", [128, 1], "float32"), "pg": ("sbuf", [128, 1], "float32"),
+    "iw": ("sbuf", [128, N * CI], "float32"), "il": ("sbuf", [128, AEND], "float32"),
+    "m1": ("sbuf", [128, 128], "float32"), "m2": ("sbuf", [128, SET1], "float32"),
+    "t1": ("sbuf", [128, 128], "float32"), "t2": ("sbuf", [128, SET1], "float32"),
+    "r1": ("sbuf", [128, 1], "float32"), "r2": ("sbuf", [128, 1], "float32"),
+    "x1": ("sbuf", [128, 1], "int32"), "x2": ("sbuf", [128, 1], "int32"),
+    "z1": ("sbuf", [128, 512], "float32"), "z2": ("sbuf", [128, 512], "float32"),
+    "y1": ("sbuf", [128, JW], "float32"), "y2": ("sbuf", [128, JW], "float32"),
+    "p1": ("psum", [128, 2048], "float32"), "p2": ("psum", [128, 1024], "float32"),
+}
+SEMAPHORES = (["d_a", "d_b", "d_sa", "d_sb", "d_pi", "d_owa", "d_owb",
+               "k_pj", "k_y",
+               "g_p", "g_c", "v_z", "v_ix", "v_oa", "v_ob", "v_ga", "v_gb", "s_ga", "s_gb", "v_qa", "v_qb",
+               "v_w", "v_oj", "v_idx", "v_c1", "s_c1", "v_c2", "s_c2", "v_y1", "s_y1", "v_y2", "s_y2",
+               "m_20", "m_21", "left", "r_an", "r_ad", "r_ar"]
+              + ["m_1%d" % n for n in range(4)] + ["r_b%d" % n for n in range(4)])
+
+
+def places(T, topo):
+    cores = list(T.cores)
+    host0 = topo.host(cores[0])
+    side = [0 if topo.host(c) == host0 else 1 for c in cores]
+    gcol = [side[:r].count(side[r]) for r in range(N)]
+    nb = [[q for q in range(N) if q != r and cores[q] in topo.cores_of(cores[r])][0] for r in range(N)]
+    direct = [[q for q in range(N) if q != r and topo.die(cores[q]) == topo.die(cores[r])] for r in range(N)]
+    return cores, side, gcol, nb, direct
+
+
+def plan(r, T, topo):
+    cores, side, gcol, nb, direct = places(T, topo)
+    c, n = cores[r], nb[r]
+    off = topo.engines(c, cores[direct[r][0]])
+    near = [e for e in topo.engines(c, cores[n]) if e not in off][:4]
+    h = len(off) // 2
+    lo, hi = off[:h], off[h:]
+    others = [q for q in range(N) if q not in (r, n)]
+
+    def far(q):
+        return side[q] != side[r] and not topo.same_plane(c, cores[q])
+
+    def apiece(q, eng, codes):
+        at = NEIGH if q == n else DIRECT + CI * direct[q].index(r)
+        return (q, eng, "r_an" if q == n else "r_ad", "qa" if codes else "za", 8 + CI * side[q], "ac" if codes else "az", at, CI)
+
+    def bpiece(q, eng, codes):
+        return (q, eng, "r_b%d" % (r // 2), "qb" if codes else "zb", CJ * gcol[q], "bc" if codes else "bz", CJ * r, CJ)
+
+    f3 = [q for q in direct[r] if far(q)][0]
+    o3 = [q for q in direct[r] if q != f3]
+    f2 = [q for q in others if far(q)]
+    mate = [q for q in others if side[q] == side[r]]
+    same = [q for q in others if q not in f2 and q not in mate]
+    a1 = [apiece(f3, lo, 1), apiece(o3[0], hi[:2], 1), apiece(o3[1], hi[2:], 1), apiece(n, near, 1)]
+    a2 = [apiece(o3[0], hi, 0), apiece(f3, lo[:2], 0), apiece(o3[1], lo[2:], 0), apiece(n, near, 0)]
+    b1 = [bpiece(f2[0], lo[:2], 1), bpiece(f2[1], lo[2:], 1)] + [bpiece(q, hi[x:x + 1], 1) for x, q in enumerate(mate + same)] + [bpiece(n, near, 1)]
+    b2 = [bpiece(same[0], hi[:2], 0), bpiece(same[1], hi[2:], 0)] + [bpiece(q, lo[x:x + 1], 0) for x, q in enumerate(f2 + mate)] + [bpiece(n, near, 0)]
+    f1 = [(n, near, "r_ar", "ac", DIRECT, "ac", RELAY, 3 * CI)]
+    f2_ = [(n, near, "r_ar", "az", DIRECT, "az", RELAY, 3 * CI)]
+    return [a1, a2, b1, b2, f1, f2_]
+
+
+def view(t, a, n):
+    v = t[:, a:a + n]
+    return v.bitcast(dt.uint8) if t.dtype != dt.uint8 else v
+
+
+def rank_program(g, core, T, topo):
+    rank = T.rank_of(core)
+    if rank is None:
+        return
+    S = T.sem
+    cores, side, gcol, nb, direct = places(T, topo)
+    calls = plan(rank, T, topo)
+    due = {}
+    for q in range(N):
+        if q != rank:
+            for call in plan(q, T, topo):
+                for w in call:
+                    if w[0] == rank:
+                        due[w[2]] = due.get(w[2], 0) + len(w[1])
+    left = sum(len(w[1]) for call in calls for w in call)
+    V, A, P, Y = g.vector, g.scalar, g.tensor, g.sync
+    COPY = ActivationFunctionType.Copy
+    own = rank // 2
+    me = side[rank]
+
+    def send(call):
+        out = []
+        for q, eng, sem, sb, sa, db, da, n in call:
+            rid, pid = topo.addr(cores[q], core)
+            out.append(RemoteDMATransfer(dst_ids=[DstId(rid=rid, pnc=pid)], dma_engine_mask=sum(1 << e for e in eng),
+                                         remote_sem=S[sem], src=view(T[sb], sa, n), dst=view(T[db], da, n)))
+        g.remote_dma_fused(out, local_sem=S.left)
+
+    def rankof(n):
+        c = cores[2 * n]
+        return 0 if n == own else 1 if side[2 * n] == me else 2 if topo.same_plane(core, c) else 3
+    order = sorted(range(4), key=rankof)
+
+    for k in range(4, 8):
+        A.dma_start(T.la[16 * k:16 * k + 16, :], T.sa[:, :]).then_inc(S.d_sa, 16)
+    for k in range(4, 8):
+        A.dma_start(T.lb[16 * k:16 * k + 16, :], T.sb[:, :]).then_inc(S.d_sb, 16)
+    A.dma_start(T.bw[:, 8:1032], T.b[:, :]).then_inc(S.d_b, 16)
+
+    for k in range(4):
+        Y.dma_start(T.la[16 * k:16 * k + 16, :], T.sa[:, :]).then_inc(S.d_sa, 16)
+    Y.dma_start(T.aw[:, 8:1032], T.a[:, :]).then_inc(S.d_a, 16)
+    for k in range(4):
+        Y.dma_start(T.lb[16 * k:16 * k + 16, :], T.sb[:, :]).then_inc(S.d_sb, 16)
+    for k in range(8):
+        Y.dma_start(T.lp[16 * k:16 * k + 16, :], T.pi[:, :]).then_inc(S.d_pi, 16)
+    o0 = 0 if me == 0 else 32
+    Y.wait_ge(S.v_qa, 1)
+    Y.dma_start(view(T.ac, OWN, 32), view(T.qa, o0, 32)).then_inc(S.d_owa, 16)
+    Y.dma_start(view(T.az, OWN, 32), view(T.za, o0, 32)).then_inc(S.d_owa, 16)
+    Y.wait_ge(S.v_qb, 1)
+    Y.dma_start(view(T.bc, CJ * rank, CJ), view(T.qb, CJ * gcol[rank], CJ)).then_inc(S.d_owb, 16)
+    Y.dma_start(view(T.bz, CJ * rank, CJ), view(T.zb, CJ * gcol[rank], CJ)).then_inc(S.d_owb, 16)
+
+    g.iota(T.ip[:, :], [[0, 1]], 0, 1).then_inc(S.g_p, 1)
+    g.iota(T.cc[:, :], [[1, AEND]], 0, 0, allow_small_or_imprecise_dtypes=True).then_inc(S.g_c, 1)
+    g.wait_ge(S.v_ix, 1)
+    g.indirect_dma_start(T.lj[:, :], None, T.pj[:, :], IndirectOffsetOnAxis(ap=T.ix[:, 0:1], axis=0), bounds_check=15).then_inc(S.k_pj, 16)
+
+    V.memset(T.aw[:, 0:8], 0.0).then_inc(S.v_z, 1)
+    V.memset(T.bw[:, 0:8], 0.0).then_inc(S.v_z, 1)
+    V.memset(T.ha[:, 0:32], 0.0).then_inc(S.v_z, 1)
+    V.memset(T.ha[:, 224:512], 0.0).then_inc(S.v_z, 1)
+    V.memset(T.iw[:, :], float(MISS)).then_inc(S.v_z, 1)
+    V.memset(T.il[:, OWN:AEND], float(MISS)).then_inc(S.v_z, 1)
+    V.wait_ge(S.g_p, 1)
+    V.tensor_scalar(T.ix[:, :], T.ip[:, :], 15, None, AluOpType.bitwise_and).then_inc(S.v_ix, 1)
+    V.wait_ge(S.d_sa, 128)
+    for t in range(4):
+        V.tensor_scalar(T.oa[:, 4 * t:4 * t + 3], T.la[:, :], 4.0, float(8 + t), AluOpType.mult, AluOpType.add).then_inc(S.v_oa, 1)
+    for q, sem in ((A, S.s_ga), (V, S.v_ga)):
+        q.wait_ge(S.v_z, 6)
+        q.wait_ge(S.v_oa, 4)
+        q.wait_ge(S.d_a, 16)
+        for t in ((0, 1) if q is A else (2, 3)):
+            o, i = T.ha[:, 32 + t:224:4], T.aw[:, 0:1032].indirect(T.oa[:, 4 * t:4 * t + 3])
+            (q.activation(o, i, COPY) if q is A else q.tensor_copy(o, i)).then_inc(sem, 1)
+    V.wait_ge(S.v_ga, 2)
+    V.wait_ge(S.s_ga, 2)
+    V.quantize_mx(T.qa[:, :], T.za[:, :], T.ha[:, :]).then_inc(S.v_qa, 1)
+    V.wait_ge(S.d_sb, 128)
+    for t in range(4):
+        V.tensor_scalar(T.ob[:, 16 * t:16 * t + 16], T.lb[:, :], 4.0, float(8 + t), AluOpType.mult, AluOpType.add).then_inc(S.v_ob, 1)
+    for q, sem in ((A, S.s_gb), (V, S.v_gb)):
+        q.wait_ge(S.v_ob, 4)
+        q.wait_ge(S.d_b, 16)
+        for t in ((0, 1) if q is A else (2, 3)):
+            o, i = T.hb[:, t:1024:4], T.bw[:, 0:1032].indirect(T.ob[:, 16 * t:16 * t + 16])
+            (q.activation(o, i, COPY) if q is A else q.tensor_copy(o, i)).then_inc(sem, 1)
+    V.wait_ge(S.v_gb, 2)
+    V.wait_ge(S.s_gb, 2)
+    V.quantize_mx(T.qb[:, :], T.zb[:, :], T.hb[:, :]).then_inc(S.v_qb, 1)
+
+    g.wait_ge(S.v_qa, 1)
+    send(calls[0])
+    send(calls[1])
+    g.wait_ge(S.v_qb, 1)
+    send(calls[2])
+    send(calls[3])
+    g.wait_ge(S.r_ad, due["r_ad"])
+    send(calls[4])
+    send(calls[5])
+
+    V.wait_ge(S.k_pj, 16)
+    V.tensor_copy(T.opj[:, :], T.lj[:, :]).then_inc(S.v_oj, 1)
+    w = [0]
+
+    def chain(inst):
+        inst.then_inc(S.v_w, 1)
+        w[0] += 1
+
+    V.wait_ge(S.g_c, 1)
+    V.wait_ge(S.d_pi, 128)
+    chain(V.tensor_copy(T.opi[:, :], T.lp[:, :]))
+    chain(V.tensor_copy(T.pf[:, :], T.ip[:, :]))
+    V.wait_ge(S.v_w, w[0])
+    chain(V.tensor_copy(T.iw[:, :].indirect(T.opi[:, :]), T.cc[:, 0:128]))
+    chain(V.tensor_scalar(T.pg[:, :], T.pf[:, :], float(SET1), None, AluOpType.add))
+    V.wait_ge(S.v_w, w[0])
+    n = nb[rank]
+    land = [(RELAY + CI * x, q) for x, q in enumerate(direct[n])] + [(NEIGH, n)]
+    land += [(DIRECT + CI * x, q) for x, q in enumerate(direct[rank])] + [(OWN + (8 if me == 0 else 0), rank)]
+    for at, q in land:
+        chain(V.tensor_copy(T.il[:, at:at + CI], T.iw[:, CI * q:CI * q + CI]))
+    chain(V.tensor_scalar(T.m1[:, :], T.cc[:, SET1:AEND], T.pg[:, 0:1], None, AluOpType.is_equal))
+    chain(V.tensor_scalar(T.m2[:, :], T.cc[:, 0:SET1], T.pf[:, 0:1], None, AluOpType.is_equal))
+    V.wait_ge(S.v_w, w[0])
+    chain(V.tensor_tensor(T.t1[:, :], T.m1[:, :], T.il[:, SET1:AEND], AluOpType.mult))
+    chain(V.tensor_tensor(T.t2[:, :], T.m2[:, :], T.il[:, 0:SET1], AluOpType.mult))
+    V.wait_ge(S.v_w, w[0])
+    chain(V.tensor_reduce(T.r1[:, :], T.t1[:, :], AxisListType.X, AluOpType.add))
+    chain(V.tensor_reduce(T.r2[:, :], T.t2[:, :], AxisListType.X, AluOpType.add))
+    V.wait_ge(S.v_w, w[0])
+    V.tensor_copy(T.x1[:, :], T.r1[:, :]).then_inc(S.v_idx, 1)
+    V.tensor_copy(T.x2[:, :], T.r2[:, :]).then_inc(S.v_idx, 1)
+
+    P.wait_ge(S.d_owa, 32)
+    P.wait_ge(S.r_an, due["r_an"])
+    P.wait_ge(S.r_ad, due["r_ad"])
+    P.wait_ge(S.d_owb, 32)
+    for x, c in enumerate(order):
+        P.wait_ge(S["r_b%d" % c], due["r_b%d" % c])
+        P.matmul_mx(T.p1[:, 512 * x:512 * x + 128], T.ac[:, SET1:AEND], T.az[:, SET1:AEND],
+                    T.bc[:, 128 * c:128 * c + 128], T.bz[:, 128 * c:128 * c + 128], True, True).then_inc(S["m_1%d" % x], 1)
+    P.wait_ge(S.r_ar, due["r_ar"])
+    for x in range(2):
+        P.matmul_mx(T.p2[:, 512 * x:512 * x + 256], T.ac[:, 0:128], T.az[:, 0:128],
+                    T.bc[:, 256 * x:256 * x + 256], T.bz[:, 256 * x:256 * x + 256], True, True).then_inc(S["m_2%d" % x], 1)
+
+    def copy(q, o, i, sem):
+        (q.activation(o, i, COPY) if q is A else q.tensor_copy(o, i)).then_inc(sem, 1)
+
+    A.wait_ge(S.v_oj, 1)
+    V.wait_ge(S.v_oj, 1)
+    for q, sem, xs in ((V, S.v_c1, (0, 2)), (A, S.s_c1, (1, 3))):
+        for x in xs:
+            c = order[x]
+            q.wait_ge(S["m_1%d" % x], 1)
+            copy(q, T.z1[:, 128 * c:128 * c + 128], T.p1[:, 512 * x:512 * x + 128], sem)
+    for q, sem, j in ((V, S.v_y1, 0), (A, S.s_y1, 12)):
+        q.wait_ge(S.v_c1, 2)
+        q.wait_ge(S.s_c1, 2)
+        copy(q, T.y1[:, 16 * j:16 * j + 192], T.z1[:, 0:512].indirect(T.opj[:, j:j + 12]), sem)
+    for q, sem, x in ((V, S.v_c2, 0), (A, S.s_c2, 1)):
+        q.wait_ge(S["m_2%d" % x], 1)
+        copy(q, T.z2[:, 256 * x:256 * x + 256], T.p2[:, 512 * x:512 * x + 256], sem)
+    for q, sem, j in ((V, S.v_y2, 0), (A, S.s_y2, 12)):
+        q.wait_ge(S.v_c2, 1)
+        q.wait_ge(S.s_c2, 1)
+        copy(q, T.y2[:, 16 * j:16 * j + 192], T.z2[:, 0:512].indirect(T.opj[:, j:j + 12]), sem)
+
+    g.wait_ge(S.v_idx, 2)
+    g.wait_ge(S.v_y1, 1)
+    g.wait_ge(S.s_y1, 1)
+    g.indirect_dma_start(T.y[:, :], IndirectOffsetOnAxis(ap=T.x1[:, 0:1], axis=0), T.y1[:, :], None, bounds_check=127, oob_is_err=False).then_inc(S.k_y, 16)
+    g.wait_ge(S.v_y2, 1)
+    g.wait_ge(S.s_y2, 1)
+    g.indirect_dma_start(T.y[:, :], IndirectOffsetOnAxis(ap=T.x2[0:SET1, 0:1], axis=0), T.y2[0:SET1, :], None, bounds_check=127, oob_is_err=False).then_inc(S.k_y, 16)
+    g.wait_ge(S.left, left)
+    g.wait_ge(S.k_y, 32)

@@ -1,41 +1,33 @@
-from concourse.bass import DstId, RemoteDMATransfer, IndirectOffsetOnAxis
-from concourse.mybir import dt, AluOpType, AxisListType, ActivationFunctionType
+from concourse.bass import DstId, RemoteDMATransfer
+from concourse.mybir import dt, AluOpType, ActivationFunctionType
 
 N, CI, CJ, JW = 8, 24, 64, 384
+NA = N * CI
 CODES = "float8_e4m3fn_x4"
-RELAY, NEIGH, DIRECT, OWN, AEND = 0, 72, 96, 168, 200
-SET1 = 72
-MISS = 1000
+HALF1, CHUNKS = 192, 320
+PAD, SPARE = 128 - CI, 304
 
 SCRATCH = {
     "aw": ("sbuf", [128, 1032], "bfloat16"), "bw": ("sbuf", [128, 1032], "bfloat16"),
-    "ha": ("sbuf", [128, 512], "bfloat16"), "hb": ("sbuf", [128, 1024], "bfloat16"),
-    "qa": ("sbuf", [128, 128], CODES), "za": ("sbuf", [128, 128], "uint8"),
-    "qb": ("sbuf", [128, 256], CODES), "zb": ("sbuf", [128, 256], "uint8"),
-    "ac": ("sbuf", [128, AEND], CODES), "az": ("sbuf", [128, AEND], "uint8"),
-    "bc": ("sbuf", [128, 512], CODES), "bz": ("sbuf", [128, 512], "uint8"),
-    "la": ("sbuf", [128, 3], "int32"), "lb": ("sbuf", [128, 16], "int32"),
-    "lp": ("sbuf", [128, 8], "int32"), "lj": ("sbuf", [128, 24], "int32"),
+    "ha": ("sbuf", [128, 1024], "bfloat16"), "h1": ("sbuf", [128, 512], "bfloat16"), "h2": ("sbuf", [128, 512], "bfloat16"),
+    "ac": ("sbuf", [128, SPARE + 128], CODES), "az": ("sbuf", [128, SPARE + 128], "uint8"),
+    "bc": ("sbuf", [128, 832], CODES), "bz": ("sbuf", [128, 832], "uint8"),
+    "la": ("sbuf", [128, 3], "int32"), "lb": ("sbuf", [128, 16], "int32"), "lq": ("sbuf", [128, 32], "int32"),
     "oa": ("sbuf", [128, 16], "uint16"), "ob": ("sbuf", [128, 64], "uint16"),
-    "opi": ("sbuf", [128, 8], "uint16"), "opj": ("sbuf", [128, 24], "uint16"),
-    "ip": ("sbuf", [128, 1], "int32"), "ix": ("sbuf", [128, 1], "int32"),
-    "cc": ("sbuf", [128, AEND], "float32"),
-    "pf": ("sbuf", [128, 1], "float32"), "pg": ("sbuf", [128, 1], "float32"),
-    "iw": ("sbuf", [128, N * CI], "float32"), "il": ("sbuf", [128, AEND], "float32"),
-    "m1": ("sbuf", [128, 128], "float32"), "m2": ("sbuf", [128, SET1], "float32"),
-    "t1": ("sbuf", [128, 128], "float32"), "t2": ("sbuf", [128, SET1], "float32"),
-    "r1": ("sbuf", [128, 1], "float32"), "r2": ("sbuf", [128, 1], "float32"),
-    "x1": ("sbuf", [128, 1], "int32"), "x2": ("sbuf", [128, 1], "int32"),
-    "z1": ("sbuf", [128, 512], "float32"), "z2": ("sbuf", [128, 512], "float32"),
-    "y1": ("sbuf", [128, JW], "float32"), "y2": ("sbuf", [128, JW], "float32"),
-    "p1": ("psum", [128, 2048], "float32"), "p2": ("psum", [128, 1024], "float32"),
+    "oi": ("sbuf", [128, 16], "uint16"), "oj": ("sbuf", [128, 24], "uint16"), "oc": ("sbuf", [128, 2], "uint16"),
+    "cq": ("sbuf", [128, 4], "int32"), "second": ("sbuf", [128, 16], "float32"), "quarter": ("sbuf", [128, 1], "float32"),
+    "ki": ("sbuf", [128, 3 * 16], "float32"), "kj": ("sbuf", [128, 6 * 24], "int32"),
+    "z0": ("sbuf", [128, 2 * NA], "float32"), "z1": ("sbuf", [128, 2 * NA], "float32"),
+    "t0": ("sbuf", [128, 256], "float32"), "t1": ("sbuf", [128, 256], "float32"),
+    "u0": ("sbuf", [128, 64], "float32"), "u1": ("sbuf", [128, 64], "float32"),
+    "rows": ("sbuf", [128, 512], "float32"), "out": ("sbuf", [128, JW], "float32"),
+    "ps": ("psum", [128, 2048], "float32"),
 }
-SEMAPHORES = (["d_a", "d_b", "d_sa", "d_sb", "d_pi", "d_owa", "d_owb",
-               "k_pj", "k_y",
-               "g_p", "g_c", "v_z", "v_ix", "v_oa", "v_ob", "v_ga", "v_gb", "s_ga", "s_gb", "v_qa", "v_qb",
-               "v_w", "v_oj", "v_idx", "v_c1", "s_c1", "v_c2", "s_c2", "v_y1", "s_y1", "v_y2", "s_y2",
-               "m_20", "m_21", "left", "r_an", "r_ad", "r_ar"]
-              + ["m_1%d" % n for n in range(4)] + ["r_b%d" % n for n in range(4)])
+SEMAPHORES = (["d_a", "d_b", "d_sa", "d_sb", "d_p", "d_y0", "d_y1", "g_c",
+               "v_z", "v_oa", "v_ob", "v_ga", "s_ga", "v_qa", "v_qo", "v_g1", "s_g1", "v_q1", "v_g2", "s_g2", "v_q2",
+               "v_w", "v_oi", "v_oj", "v_f", "s_f", "v_y", "s_y", "left", "r_ad", "r_ar"]
+              + ["%s%d" % (s, n) for s in ("m", "r_b") for n in range(4)]
+              + ["%s%d" % (s, n) for s in ("cp", "vg", "sg", "vt") for n in range(2)])
 
 
 def places(T, topo):
@@ -44,41 +36,68 @@ def places(T, topo):
     side = [0 if topo.host(c) == host0 else 1 for c in cores]
     gcol = [side[:r].count(side[r]) for r in range(N)]
     nb = [[q for q in range(N) if q != r and cores[q] in topo.cores_of(cores[r])][0] for r in range(N)]
-    direct = [[q for q in range(N) if q != r and topo.die(cores[q]) == topo.die(cores[r])] for r in range(N)]
-    return cores, side, gcol, nb, direct
+    assert all(nb[r] // 2 == r // 2 for r in range(N))
+    return cores, side, gcol, nb
+
+
+def a_at(r, q, nb):
+    return (PAD if r > nb[r] else 8) + CI * ((q - max(r, nb[r])) % N)
+
+
+def a_run(r, nb):
+    return [(r + x) % N for x in (range(4) if r > nb[r] else range(-3, 1))]
+
+
+def a_tiles(r, side, nb):
+    mine = PAD + CI * side[r]
+    start = mine - PAD if r > nb[r] else mine
+    tile = (start, a_at(r, r, nb) - (mine - start))
+    return [tile] if start <= PAD and start + 128 >= PAD + 2 * CI else [(PAD, SPARE), tile]
+
+
+def b_layout(r, gcol, nb):
+    return (CJ, 0) if gcol[r] < gcol[nb[r]] else (0, CJ)
+
+
+def b_at(r, q, gcol, nb):
+    base = b_layout(r, gcol, nb)[1] if q // 2 == r // 2 else CHUNKS + 128 * (q // 2)
+    return base + CJ * (1 - q % 2)
 
 
 def plan(r, T, topo):
-    cores, side, gcol, nb, direct = places(T, topo)
+    cores, side, gcol, nb = places(T, topo)
     c, n = cores[r], nb[r]
-    off = topo.engines(c, cores[direct[r][0]])
-    near = [e for e in topo.engines(c, cores[n]) if e not in off][:4]
-    h = len(off) // 2
-    lo, hi = off[:h], off[h:]
     others = [q for q in range(N) if q not in (r, n)]
-
-    def far(q):
-        return side[q] != side[r] and not topo.same_plane(c, cores[q])
-
-    def apiece(q, eng, codes):
-        at = NEIGH if q == n else DIRECT + CI * direct[q].index(r)
-        return (q, eng, "r_an" if q == n else "r_ad", "qa" if codes else "za", 8 + CI * side[q], "ac" if codes else "az", at, CI)
-
-    def bpiece(q, eng, codes):
-        return (q, eng, "r_b%d" % (r // 2), "qb" if codes else "zb", CJ * gcol[q], "bc" if codes else "bz", CJ * r, CJ)
-
-    f3 = [q for q in direct[r] if far(q)][0]
-    o3 = [q for q in direct[r] if q != f3]
-    f2 = [q for q in others if far(q)]
+    off = topo.engines(c, cores[others[0]])
+    near = [e for e in topo.engines(c, cores[n]) if e not in off]
+    nc, nz = near[0::2], near[1::2]
+    h = len(off) // 2
+    lo, hi, ev, od = off[:h], off[h:], off[0::2], off[1::2]
     mate = [q for q in others if side[q] == side[r]]
-    same = [q for q in others if q not in f2 and q not in mate]
-    a1 = [apiece(f3, lo, 1), apiece(o3[0], hi[:2], 1), apiece(o3[1], hi[2:], 1), apiece(n, near, 1)]
-    a2 = [apiece(o3[0], hi, 0), apiece(f3, lo[:2], 0), apiece(o3[1], lo[2:], 0), apiece(n, near, 0)]
-    b1 = [bpiece(f2[0], lo[:2], 1), bpiece(f2[1], lo[2:], 1)] + [bpiece(q, hi[x:x + 1], 1) for x, q in enumerate(mate + same)] + [bpiece(n, near, 1)]
-    b2 = [bpiece(same[0], hi[:2], 0), bpiece(same[1], hi[2:], 0)] + [bpiece(q, lo[x:x + 1], 0) for x, q in enumerate(f2 + mate)] + [bpiece(n, near, 0)]
-    f1 = [(n, near, "r_ar", "ac", DIRECT, "ac", RELAY, 3 * CI)]
-    f2_ = [(n, near, "r_ar", "az", DIRECT, "az", RELAY, 3 * CI)]
-    return [a1, a2, b1, b2, f1, f2_]
+    plane = [q for q in others if topo.same_plane(c, cores[q])]
+    far = [q for q in others if q not in mate + plane]
+    inha, inac = a_tiles(r, side, nb)[0]
+
+    def apiece(q, eng, buf):
+        return (q, eng, "r_ad", buf, inac + PAD - inha + CI * side[q], a_at(q, r, nb), CI)
+
+    def bpiece(q, eng, buf):
+        here = b_layout(r, gcol, nb)[0] if gcol[q] // 2 == gcol[r] // 2 else HALF1
+        return (q, eng, "r_b%d" % (r // 2), buf, here + CJ * (gcol[q] % 2), b_at(q, r, gcol, nb), CJ)
+
+    af, ap, am = [[q for q in pair if r in a_run(q, nb)][0] for pair in (far, plane, mate)]
+    head = a_run(r, nb)[0]
+    return {
+        "a codes": [apiece(af, lo, "ac"), apiece(ap, hi[:2], "ac"), apiece(am, hi[2:], "ac")],
+        "a scales": [apiece(ap, hi, "az"), apiece(af, lo[:2], "az"), apiece(am, lo[2:], "az")],
+        "mate codes": [bpiece(mate[0], ev[:2], "bc"), bpiece(mate[1], ev[2:], "bc")],
+        "first scales": [bpiece(q, (ev + od)[2 * x:2 * x + 2], "bz") for x, q in enumerate(mate + far)],
+        "far codes": [bpiece(far[0], lo, "bc"), bpiece(far[1], hi, "bc")],
+        "second scales": [bpiece(plane[0], lo, "bz"), bpiece(plane[1], hi, "bz"), bpiece(n, nz, "bz")],
+        "plane codes": [bpiece(plane[0], od[:2], "bc"), bpiece(plane[1], od[2:], "bc"), bpiece(n, nc, "bc")],
+        "on codes": [(n, near, "r_ar", "ac", a_at(r, head, nb), a_at(n, head, nb), 4 * CI)],
+        "on scales": [(n, near, "r_ar", "az", a_at(r, head, nb), a_at(n, head, nb), 4 * CI)],
+    }, [r // 2, mate[0] // 2, plane[0] // 2, far[0] // 2]
 
 
 def view(t, a, n):
@@ -91,178 +110,206 @@ def rank_program(g, core, T, topo):
     if rank is None:
         return
     S = T.sem
-    cores, side, gcol, nb, direct = places(T, topo)
-    calls = plan(rank, T, topo)
+    cores, side, gcol, nb = places(T, topo)
+    calls, order = plan(rank, T, topo)
     due = {}
     for q in range(N):
         if q != rank:
-            for call in plan(q, T, topo):
+            for call in plan(q, T, topo)[0].values():
                 for w in call:
                     if w[0] == rank:
                         due[w[2]] = due.get(w[2], 0) + len(w[1])
-    left = sum(len(w[1]) for call in calls for w in call)
+    left = sum(len(w[1]) for call in calls.values() for w in call)
     V, A, P, Y = g.vector, g.scalar, g.tensor, g.sync
     COPY = ActivationFunctionType.Copy
-    own = rank // 2
-    me = side[rank]
+    OP = AluOpType
+    lead = max(rank, nb[rank])
+    afirst = a_at(rank, lead, nb)
+    btile, bown = b_layout(rank, gcol, nb)
 
-    def send(call):
+    def send(name):
         out = []
-        for q, eng, sem, sb, sa, db, da, n in call:
+        for q, eng, sem, buf, here, there, n in calls[name]:
             rid, pid = topo.addr(cores[q], core)
             out.append(RemoteDMATransfer(dst_ids=[DstId(rid=rid, pnc=pid)], dma_engine_mask=sum(1 << e for e in eng),
-                                         remote_sem=S[sem], src=view(T[sb], sa, n), dst=view(T[db], da, n)))
+                                         remote_sem=S[sem], src=view(T[buf], here, n), dst=view(T[buf], there, n)))
         g.remote_dma_fused(out, local_sem=S.left)
 
-    def rankof(n):
-        c = cores[2 * n]
-        return 0 if n == own else 1 if side[2 * n] == me else 2 if topo.same_plane(core, c) else 3
-    order = sorted(range(4), key=rankof)
+    def copy(q, o, i, sem):
+        (q.activation(o, i, COPY) if q is A else q.tensor_copy(o, i)).then_inc(sem, 1)
+
+    def part(a, n=1):
+        return slice(32 * a, 32 * (a + n))
+
+    w = [0]
+
+    def step(*insts):
+        if w[0]:
+            V.wait_ge(S.v_w, w[0])
+        for inst in insts:
+            inst().then_inc(S.v_w, 1)
+        w[0] += len(insts)
+
+    def scalar(o, i, *ops):
+        return lambda: V.tensor_scalar(o, i, *ops)
+
+    def add(o, i, j):
+        return lambda: V.tensor_tensor(o, i, j, OP.add)
 
     for k in range(4, 8):
         A.dma_start(T.la[16 * k:16 * k + 16, :], T.sa[:, :]).then_inc(S.d_sa, 16)
     for k in range(4, 8):
         A.dma_start(T.lb[16 * k:16 * k + 16, :], T.sb[:, :]).then_inc(S.d_sb, 16)
     A.dma_start(T.bw[:, 8:1032], T.b[:, :]).then_inc(S.d_b, 16)
-
     for k in range(4):
         Y.dma_start(T.la[16 * k:16 * k + 16, :], T.sa[:, :]).then_inc(S.d_sa, 16)
     Y.dma_start(T.aw[:, 8:1032], T.a[:, :]).then_inc(S.d_a, 16)
     for k in range(4):
         Y.dma_start(T.lb[16 * k:16 * k + 16, :], T.sb[:, :]).then_inc(S.d_sb, 16)
-    for k in range(8):
-        Y.dma_start(T.lp[16 * k:16 * k + 16, :], T.pi[:, :]).then_inc(S.d_pi, 16)
-    o0 = 0 if me == 0 else 32
-    Y.wait_ge(S.v_qa, 1)
-    Y.dma_start(view(T.ac, OWN, 32), view(T.qa, o0, 32)).then_inc(S.d_owa, 16)
-    Y.dma_start(view(T.az, OWN, 32), view(T.za, o0, 32)).then_inc(S.d_owa, 16)
-    Y.wait_ge(S.v_qb, 1)
-    Y.dma_start(view(T.bc, CJ * rank, CJ), view(T.qb, CJ * gcol[rank], CJ)).then_inc(S.d_owb, 16)
-    Y.dma_start(view(T.bz, CJ * rank, CJ), view(T.zb, CJ * gcol[rank], CJ)).then_inc(S.d_owb, 16)
+    for k in range(2):
+        Y.dma_start(T.lq[16 * k:16 * k + 16, 0:8], T.pi[:, :]).then_inc(S.d_p, 16)
+        Y.dma_start(T.lq[16 * k:16 * k + 16, 8:32], T.pj[:, :]).then_inc(S.d_p, 16)
 
-    g.iota(T.ip[:, :], [[0, 1]], 0, 1).then_inc(S.g_p, 1)
-    g.iota(T.cc[:, :], [[1, AEND]], 0, 0, allow_small_or_imprecise_dtypes=True).then_inc(S.g_c, 1)
-    g.wait_ge(S.v_ix, 1)
-    g.indirect_dma_start(T.lj[:, :], None, T.pj[:, :], IndirectOffsetOnAxis(ap=T.ix[:, 0:1], axis=0), bounds_check=15).then_inc(S.k_pj, 16)
+    for a in range(4):
+        g.iota(T.cq[part(a), 0:1], [[0, 1]], 4 * a, 1).then_inc(S.g_c, 1)
+    g.wait_ge(S.g_c, 4)
+    g.iota(T.second[:, :], [[0, 4], [NA, 2], [0, 2]], -CI * lead, 0, allow_small_or_imprecise_dtypes=True).then_inc(S.g_c, 1)
+    for z in (T.aw[:, 0:8], T.bw[:, 0:8], T.ha[:, 0:4 * PAD], T.ha[:, 4 * (PAD + 2 * CI):1024]):
+        V.memset(z, 0.0).then_inc(S.v_z, 1)
+    for b in range(4):
+        V.memset(T.quarter[part(b), :], float(64 * b + 128 + 63 + 1024)).then_inc(S.v_z, 1)
+    V.wait_ge(S.g_c, 4)
+    step(scalar(T.cq[:, 1:2], T.cq[:, 0:1], 1, 6, OP.logical_shift_right, OP.bitwise_and),
+         scalar(T.cq[:, 2:3], T.cq[:, 0:1], 1, None, OP.bitwise_and))
+    step(add(T.cq[:, 3:4], T.cq[:, 1:2], T.cq[:, 2:3]))
+    step(lambda: V.tensor_copy(T.oc[:, 0:1], T.cq[:, 3:4]))
 
-    V.memset(T.aw[:, 0:8], 0.0).then_inc(S.v_z, 1)
-    V.memset(T.bw[:, 0:8], 0.0).then_inc(S.v_z, 1)
-    V.memset(T.ha[:, 0:32], 0.0).then_inc(S.v_z, 1)
-    V.memset(T.ha[:, 224:512], 0.0).then_inc(S.v_z, 1)
-    V.memset(T.iw[:, :], float(MISS)).then_inc(S.v_z, 1)
-    V.memset(T.il[:, OWN:AEND], float(MISS)).then_inc(S.v_z, 1)
-    V.wait_ge(S.g_p, 1)
-    V.tensor_scalar(T.ix[:, :], T.ip[:, :], 15, None, AluOpType.bitwise_and).then_inc(S.v_ix, 1)
     V.wait_ge(S.d_sa, 128)
     for t in range(4):
-        V.tensor_scalar(T.oa[:, 4 * t:4 * t + 3], T.la[:, :], 4.0, float(8 + t), AluOpType.mult, AluOpType.add).then_inc(S.v_oa, 1)
+        V.tensor_scalar(T.oa[:, 4 * t:4 * t + 3], T.la[:, :], 4.0, float(8 + t), OP.mult, OP.add).then_inc(S.v_oa, 1)
     for q, sem in ((A, S.s_ga), (V, S.v_ga)):
-        q.wait_ge(S.v_z, 6)
+        q.wait_ge(S.v_z, 8)
         q.wait_ge(S.v_oa, 4)
         q.wait_ge(S.d_a, 16)
         for t in ((0, 1) if q is A else (2, 3)):
-            o, i = T.ha[:, 32 + t:224:4], T.aw[:, 0:1032].indirect(T.oa[:, 4 * t:4 * t + 3])
-            (q.activation(o, i, COPY) if q is A else q.tensor_copy(o, i)).then_inc(sem, 1)
+            copy(q, T.ha[:, 4 * PAD + t:4 * (PAD + 2 * CI):4], T.aw[:, 0:1032].indirect(T.oa[:, 4 * t:4 * t + 3]), sem)
     V.wait_ge(S.v_ga, 2)
     V.wait_ge(S.s_ga, 2)
-    V.quantize_mx(T.qa[:, :], T.za[:, :], T.ha[:, :]).then_inc(S.v_qa, 1)
+    tiles = a_tiles(rank, side, nb)
+    for (inha, inac), sem in zip(tiles, (S.v_qa, S.v_qo)):
+        V.quantize_mx(T.ac[:, inac:inac + 128], T.az[:, inac:inac + 128], T.ha[:, 4 * inha:4 * inha + 512]).then_inc(sem, 1)
+
+    def ki(x):
+        return T.ki[:, 16 * x:16 * x + 16]
+
+    def kj(x):
+        return T.kj[:, 24 * x:24 * x + 24]
+
+    def gather(q, x, ts):
+        pair = gcol[rank] // 2 if x == 2 else 1 - gcol[rank] // 2
+        for t in ts:
+            o = 16 * t + 8 * pair
+            copy(q, T["h%d" % x][:, t:512:4], T.bw[:, 0:1032].indirect(T.ob[:, o:o + 8]), S["%s_g%d" % ("s" if q is A else "v", x)])
+
+    def quantise(x, at, nv):
+        V.wait_ge(S["v_g%d" % x], nv)
+        V.wait_ge(S["s_g%d" % x], 4 - nv)
+        V.quantize_mx(T.bc[:, at:at + 128], T.bz[:, at:at + 128], T["h%d" % x][:, :]).then_inc(S["v_q%d" % x], 1)
+
     V.wait_ge(S.d_sb, 128)
     for t in range(4):
-        V.tensor_scalar(T.ob[:, 16 * t:16 * t + 16], T.lb[:, :], 4.0, float(8 + t), AluOpType.mult, AluOpType.add).then_inc(S.v_ob, 1)
-    for q, sem in ((A, S.s_gb), (V, S.v_gb)):
+        V.tensor_scalar(T.ob[:, 16 * t:16 * t + 16], T.lb[:, :], 4.0, float(8 + t), OP.mult, OP.add).then_inc(S.v_ob, 1)
+    for q in (A, V):
         q.wait_ge(S.v_ob, 4)
         q.wait_ge(S.d_b, 16)
-        for t in ((0, 1) if q is A else (2, 3)):
-            o, i = T.hb[:, t:1024:4], T.bw[:, 0:1032].indirect(T.ob[:, 16 * t:16 * t + 16])
-            (q.activation(o, i, COPY) if q is A else q.tensor_copy(o, i)).then_inc(sem, 1)
-    V.wait_ge(S.v_gb, 2)
-    V.wait_ge(S.s_gb, 2)
-    V.quantize_mx(T.qb[:, :], T.zb[:, :], T.hb[:, :]).then_inc(S.v_qb, 1)
+    gather(A, 1, (0, 1))
+    gather(A, 2, (0, 1, 2))
+    gather(V, 1, (2, 3))
+    quantise(1, HALF1, 2)
+    V.wait_ge(S.g_c, 5)
+    V.wait_ge(S.d_p, 64)
+    step(lambda: V.tensor_copy(T.lq[part(1), :], T.lq[part(0), :]))
+    gather(V, 2, (3,))
+    step(lambda: V.tensor_copy(T.lq[part(2, 2), :], T.lq[part(0, 2), :]))
+    picked, lj = T.lq[:, 0:8].indirect(T.oc[:, 0:1]), T.lq[:, 8:32]
+    step(add(ki(0), picked, T.second[:, :]),
+         scalar(ki(1), picked, float(CI * lead), float(NA), OP.is_lt, OP.mult),
+         scalar(kj(0), lj, -2.0, T.quarter[:, 0:1], OP.mult, OP.add))
+    quantise(2, btile, 1)
+    step(add(ki(2), ki(0), ki(1)),
+         scalar(kj(1), lj, 256 + 31, None, OP.bitwise_and),
+         scalar(kj(2), lj, 2, 32, OP.logical_shift_right, OP.bitwise_and),
+         scalar(kj(3), kj(0), 192, None, OP.bitwise_and))
+    step(add(kj(4), kj(1), kj(2)))
+    V.tensor_copy(T.oi[:, :], ki(2)).then_inc(S.v_oi, 1)
+    step(add(kj(5), kj(4), kj(3)))
+    step()
+    V.tensor_copy(T.oj[:, :], kj(5)).then_inc(S.v_oj, 1)
 
     g.wait_ge(S.v_qa, 1)
-    send(calls[0])
-    send(calls[1])
-    g.wait_ge(S.v_qb, 1)
-    send(calls[2])
-    send(calls[3])
+    send("a codes")
+    send("a scales")
+    g.wait_ge(S.v_q1, 1)
+    send("mate codes")
+    send("first scales")
+    g.wait_ge(S.v_q2, 1)
+    send("plane codes")
+    send("second scales")
+    send("far codes")
+    if len(tiles) == 2:
+        g.wait_ge(S.v_qo, 1)
     g.wait_ge(S.r_ad, due["r_ad"])
-    send(calls[4])
-    send(calls[5])
-
-    V.wait_ge(S.k_pj, 16)
-    V.tensor_copy(T.opj[:, :], T.lj[:, :]).then_inc(S.v_oj, 1)
-    w = [0]
-
-    def chain(inst):
-        inst.then_inc(S.v_w, 1)
-        w[0] += 1
-
-    V.wait_ge(S.g_c, 1)
-    V.wait_ge(S.d_pi, 128)
-    chain(V.tensor_copy(T.opi[:, :], T.lp[:, :]))
-    chain(V.tensor_copy(T.pf[:, :], T.ip[:, :]))
-    V.wait_ge(S.v_w, w[0])
-    chain(V.tensor_copy(T.iw[:, :].indirect(T.opi[:, :]), T.cc[:, 0:128]))
-    chain(V.tensor_scalar(T.pg[:, :], T.pf[:, :], float(SET1), None, AluOpType.add))
-    V.wait_ge(S.v_w, w[0])
-    n = nb[rank]
-    land = [(RELAY + CI * x, q) for x, q in enumerate(direct[n])] + [(NEIGH, n)]
-    land += [(DIRECT + CI * x, q) for x, q in enumerate(direct[rank])] + [(OWN + (8 if me == 0 else 0), rank)]
-    for at, q in land:
-        chain(V.tensor_copy(T.il[:, at:at + CI], T.iw[:, CI * q:CI * q + CI]))
-    chain(V.tensor_scalar(T.m1[:, :], T.cc[:, SET1:AEND], T.pg[:, 0:1], None, AluOpType.is_equal))
-    chain(V.tensor_scalar(T.m2[:, :], T.cc[:, 0:SET1], T.pf[:, 0:1], None, AluOpType.is_equal))
-    V.wait_ge(S.v_w, w[0])
-    chain(V.tensor_tensor(T.t1[:, :], T.m1[:, :], T.il[:, SET1:AEND], AluOpType.mult))
-    chain(V.tensor_tensor(T.t2[:, :], T.m2[:, :], T.il[:, 0:SET1], AluOpType.mult))
-    V.wait_ge(S.v_w, w[0])
-    chain(V.tensor_reduce(T.r1[:, :], T.t1[:, :], AxisListType.X, AluOpType.add))
-    chain(V.tensor_reduce(T.r2[:, :], T.t2[:, :], AxisListType.X, AluOpType.add))
-    V.wait_ge(S.v_w, w[0])
-    V.tensor_copy(T.x1[:, :], T.r1[:, :]).then_inc(S.v_idx, 1)
-    V.tensor_copy(T.x2[:, :], T.r2[:, :]).then_inc(S.v_idx, 1)
-
-    P.wait_ge(S.d_owa, 32)
-    P.wait_ge(S.r_an, due["r_an"])
-    P.wait_ge(S.r_ad, due["r_ad"])
-    P.wait_ge(S.d_owb, 32)
-    for x, c in enumerate(order):
-        P.wait_ge(S["r_b%d" % c], due["r_b%d" % c])
-        P.matmul_mx(T.p1[:, 512 * x:512 * x + 128], T.ac[:, SET1:AEND], T.az[:, SET1:AEND],
-                    T.bc[:, 128 * c:128 * c + 128], T.bz[:, 128 * c:128 * c + 128], True, True).then_inc(S["m_1%d" % x], 1)
-    P.wait_ge(S.r_ar, due["r_ar"])
-    for x in range(2):
-        P.matmul_mx(T.p2[:, 512 * x:512 * x + 256], T.ac[:, 0:128], T.az[:, 0:128],
-                    T.bc[:, 256 * x:256 * x + 256], T.bz[:, 256 * x:256 * x + 256], True, True).then_inc(S["m_2%d" % x], 1)
-
-    def copy(q, o, i, sem):
-        (q.activation(o, i, COPY) if q is A else q.tensor_copy(o, i)).then_inc(sem, 1)
-
-    A.wait_ge(S.v_oj, 1)
-    V.wait_ge(S.v_oj, 1)
-    for q, sem, xs in ((V, S.v_c1, (0, 2)), (A, S.s_c1, (1, 3))):
-        for x in xs:
-            c = order[x]
-            q.wait_ge(S["m_1%d" % x], 1)
-            copy(q, T.z1[:, 128 * c:128 * c + 128], T.p1[:, 512 * x:512 * x + 128], sem)
-    for q, sem, j in ((V, S.v_y1, 0), (A, S.s_y1, 12)):
-        q.wait_ge(S.v_c1, 2)
-        q.wait_ge(S.s_c1, 2)
-        copy(q, T.y1[:, 16 * j:16 * j + 192], T.z1[:, 0:512].indirect(T.opj[:, j:j + 12]), sem)
-    for q, sem, x in ((V, S.v_c2, 0), (A, S.s_c2, 1)):
-        q.wait_ge(S["m_2%d" % x], 1)
-        copy(q, T.z2[:, 256 * x:256 * x + 256], T.p2[:, 512 * x:512 * x + 256], sem)
-    for q, sem, j in ((V, S.v_y2, 0), (A, S.s_y2, 12)):
-        q.wait_ge(S.v_c2, 1)
-        q.wait_ge(S.s_c2, 1)
-        copy(q, T.y2[:, 16 * j:16 * j + 192], T.z2[:, 0:512].indirect(T.opj[:, j:j + 12]), sem)
-
-    g.wait_ge(S.v_idx, 2)
-    g.wait_ge(S.v_y1, 1)
-    g.wait_ge(S.s_y1, 1)
-    g.indirect_dma_start(T.y[:, :], IndirectOffsetOnAxis(ap=T.x1[:, 0:1], axis=0), T.y1[:, :], None, bounds_check=127, oob_is_err=False).then_inc(S.k_y, 16)
-    g.wait_ge(S.v_y2, 1)
-    g.wait_ge(S.s_y2, 1)
-    g.indirect_dma_start(T.y[:, :], IndirectOffsetOnAxis(ap=T.x2[0:SET1, 0:1], axis=0), T.y2[0:SET1, :], None, bounds_check=127, oob_is_err=False).then_inc(S.k_y, 16)
+    send("on codes")
+    send("on scales")
     g.wait_ge(S.left, left)
-    g.wait_ge(S.k_y, 32)
+
+    P.wait_ge(S.v_qa, 1)
+    P.wait_ge(S.v_q2, 1)
+    if len(tiles) == 2:
+        P.wait_ge(S.v_qo, 1)
+    for sem in ("r_ad", "r_ar"):
+        P.wait_ge(S[sem], due[sem])
+    for x, c in enumerate(order):
+        at = bown if x == 0 else CHUNKS + 128 * c
+        P.wait_ge(S["r_b%d" % c], due["r_b%d" % c])
+        P.matmul_mx(T.ps[:, 512 * x:512 * x + NA], T.bc[:, at:at + 128], T.bz[:, at:at + 128],
+                    T.ac[:, afirst:afirst + NA], T.az[:, afirst:afirst + NA], True, True).then_inc(S["m%d" % x], 1)
+
+    for q in (V, A):
+        q.wait_ge(S.v_oi, 1)
+    for n in range(2):
+        z, t, u = T["z%d" % n], T["t%d" % n], T["u%d" % n]
+        cp, vg, sg, vt = [S["%s%d" % (s, n)] for s in ("cp", "vg", "sg", "vt")]
+        col = 256 * (order[2 * n] // 2)
+        for q, x in ((A, 2 * n), (V, 2 * n + 1)):
+            at = NA * (order[x] % 2)
+            q.wait_ge(S["m%d" % x], 1)
+            copy(q, z[:, at:at + NA], T.ps[:, 512 * x:512 * x + NA], cp)
+        for q, sem, hf in ((V, vg, 0), (A, sg, 1)):
+            q.wait_ge(cp, 2)
+            copy(q, t[:, 128 * hf:128 * hf + 128], z[:, :].indirect(T.oi[:, 8 * hf:8 * hf + 8]), sem)
+
+        def turn(s, a, m):
+            V.transpose(T.rows[part((a + s) % 4, m), col + 64 * s:col + 64 * s + 64], t[part(a, m), 64 * s:64 * s + 64]).then_inc(S.v_f, 1)
+
+        V.wait_ge(vg, 1)
+        V.transpose(u[:, :], t[:, 64:128]).then_inc(vt, 1)
+        turn(0, 0, 4)
+        V.wait_ge(sg, 1)
+        turn(2, 0, 2)
+        turn(2, 2, 2)
+        for a in range(4):
+            turn(3, a, 1)
+        A.wait_ge(vt, 1)
+        for a in range(4):
+            copy(A, T.rows[part((a + 1) % 4), col + 64:col + 128], u[part(a), :], S.s_f)
+
+    for q, sem, j in ((V, S.v_y, 0), (A, S.s_y, 12)):
+        q.wait_ge(S.v_oj, 1)
+        q.wait_ge(S.v_f, 14)
+        q.wait_ge(S.s_f, 8)
+        copy(q, T.out[:, 16 * j:16 * j + 192], T.rows[:, 0:512].indirect(T.oj[:, j:j + 12]), sem)
+    for q, sem, done, j in ((Y, S.v_y, S.d_y0, 0), (A, S.s_y, S.d_y1, 192)):
+        q.wait_ge(sem, 1)
+        q.dma_start(T.y[:, j:j + 192], T.out[:, j:j + 192]).then_inc(done, 16)
+        q.wait_ge(done, 16)

@@ -6,6 +6,7 @@ NA = N * CI
 CODES = "float8_e4m3fn_x4"
 HALF1, CHUNKS = 192, 320
 PAD, SPARE = 128 - CI, 304
+HELPED = ("mate scales", "mate codes")
 
 SCRATCH = {
     "aw": ("sbuf", [128, 1032], "bfloat16"), "bw": ("sbuf", [128, 1032], "bfloat16"),
@@ -16,17 +17,17 @@ SCRATCH = {
     "oa": ("sbuf", [128, 16], "uint16"), "ob": ("sbuf", [128, 64], "uint16"),
     "oi": ("sbuf", [128, 16], "uint16"), "oj": ("sbuf", [128, 24], "uint16"), "oc": ("sbuf", [128, 2], "uint16"),
     "cq": ("sbuf", [128, 4], "int32"), "second": ("sbuf", [128, 16], "float32"), "quarter": ("sbuf", [128, 1], "float32"),
-    "ki": ("sbuf", [128, 3 * 16], "float32"), "kj": ("sbuf", [128, 6 * 24], "int32"),
+    "ki": ("sbuf", [128, 3 * 16], "float32"), "kj": ("sbuf", [128, 7 * 24], "int32"),
     "z0": ("sbuf", [128, 2 * NA], "float32"), "z1": ("sbuf", [128, 2 * NA], "float32"),
     "t0": ("sbuf", [128, 256], "float32"), "t1": ("sbuf", [128, 256], "float32"),
     "u0": ("sbuf", [128, 64], "float32"), "u1": ("sbuf", [128, 64], "float32"),
     "rows": ("sbuf", [128, 512], "float32"), "out": ("sbuf", [128, JW], "float32"),
-    "ps": ("psum", [128, 2048], "float32"),
+    "ps": ("psum", [128, 3072], "float32"),
 }
 SEMAPHORES = (["d_a", "d_b", "d_sa", "d_sb", "d_p", "d_y0", "d_y1", "g_c",
                "v_z", "v_oa", "v_ob", "v_ga", "s_ga", "v_qa", "v_qo", "v_g1", "s_g1", "v_q1", "v_g2", "s_g2", "v_q2",
-               "v_w", "v_oi", "v_oj", "v_f", "s_f", "v_y", "s_y", "left", "r_ad", "r_ar"]
-              + ["%s%d" % (s, n) for s in ("m", "r_b") for n in range(4)]
+               "v_w", "v_oi", "v_oj", "v_f", "s_f", "y0", "y1", "left", "r_ac", "r_az", "r_ar"]
+              + ["m%d" % n for n in range(6)] + ["r_b%d" % n for n in range(4)]
               + ["%s%d" % (s, n) for s in ("cp", "vg", "sg", "vt") for n in range(2)])
 
 
@@ -37,6 +38,9 @@ def places(T, topo):
     gcol = [side[:r].count(side[r]) for r in range(N)]
     nb = [[q for q in range(N) if q != r and cores[q] in topo.cores_of(cores[r])][0] for r in range(N)]
     assert all(nb[r] // 2 == r // 2 for r in range(N))
+    for c in cores[:N]:
+        cores.append([h for h in topo.cores_of(c) if h not in cores and topo.die(h) == topo.die(c)
+                      and all(topo.may_write(h, d) for d in cores[:N])][0])
     return cores, side, gcol, nb
 
 
@@ -70,7 +74,7 @@ def plan(r, T, topo):
     others = [q for q in range(N) if q not in (r, n)]
     off = topo.engines(c, cores[others[0]])
     near = [e for e in topo.engines(c, cores[n]) if e not in off]
-    nc, nz = near[0::2], near[1::2]
+    nc, nz = near, near
     h = len(off) // 2
     lo, hi, ev, od = off[:h], off[h:], off[0::2], off[1::2]
     mate = [q for q in others if side[q] == side[r]]
@@ -79,7 +83,7 @@ def plan(r, T, topo):
     inha, inac = a_tiles(r, side, nb)[0]
 
     def apiece(q, eng, buf):
-        return (q, eng, "r_ad", buf, inac + PAD - inha + CI * side[q], a_at(q, r, nb), CI)
+        return (q, eng, "r_" + buf, buf, inac + PAD - inha + CI * side[q], a_at(q, r, nb), CI)
 
     def bpiece(q, eng, buf):
         here = b_layout(r, gcol, nb)[0] if gcol[q] // 2 == gcol[r] // 2 else HALF1
@@ -90,14 +94,17 @@ def plan(r, T, topo):
     return {
         "a codes": [apiece(af, lo, "ac"), apiece(ap, hi[:2], "ac"), apiece(am, hi[2:], "ac")],
         "a scales": [apiece(ap, hi, "az"), apiece(af, lo[:2], "az"), apiece(am, lo[2:], "az")],
-        "mate codes": [bpiece(mate[0], ev[:2], "bc"), bpiece(mate[1], ev[2:], "bc")],
-        "first scales": [bpiece(q, (ev + od)[2 * x:2 * x + 2], "bz") for x, q in enumerate(mate + far)],
+        "help codes": [(N + r, nc, "r_ac", "bc", HALF1, HALF1, 2 * CJ)],
+        "help scales": [(N + r, nz, "r_az", "bz", HALF1, HALF1, 2 * CJ)],
+        "mate codes": [bpiece(mate[0], lo, "bc"), bpiece(mate[1], hi, "bc")],
+        "mate scales": [bpiece(mate[0], lo, "bz"), bpiece(mate[1], hi, "bz")],
         "far codes": [bpiece(far[0], lo, "bc"), bpiece(far[1], hi, "bc")],
+        "far scales": [bpiece(far[0], lo, "bz"), bpiece(far[1], hi, "bz")],
         "second scales": [bpiece(plane[0], lo, "bz"), bpiece(plane[1], hi, "bz"), bpiece(n, nz, "bz")],
-        "plane codes": [bpiece(plane[0], od[:2], "bc"), bpiece(plane[1], od[2:], "bc"), bpiece(n, nc, "bc")],
+        "plane codes": [bpiece(plane[0], lo, "bc"), bpiece(plane[1], hi, "bc"), bpiece(n, nc, "bc")],
         "on codes": [(n, near, "r_ar", "ac", a_at(r, head, nb), a_at(n, head, nb), 4 * CI)],
         "on scales": [(n, near, "r_ar", "az", a_at(r, head, nb), a_at(n, head, nb), 4 * CI)],
-    }, [r // 2, mate[0] // 2, plane[0] // 2, far[0] // 2]
+    }, [r // 2, far[0] // 2, plane[0] // 2, mate[0] // 2]
 
 
 def view(t, a, n):
@@ -106,20 +113,20 @@ def view(t, a, n):
 
 
 def rank_program(g, core, T, topo):
-    rank = T.rank_of(core)
-    if rank is None:
-        return
     S = T.sem
     cores, side, gcol, nb = places(T, topo)
+    if core not in cores:
+        return
+    me = cores.index(core)
+    rank = me % N
     calls, order = plan(rank, T, topo)
     due = {}
     for q in range(N):
-        if q != rank:
-            for call in plan(q, T, topo)[0].values():
-                for w in call:
-                    if w[0] == rank:
-                        due[w[2]] = due.get(w[2], 0) + len(w[1])
-    left = sum(len(w[1]) for call in calls.values() for w in call)
+        for call in plan(q, T, topo)[0].values():
+            for w in call:
+                if w[0] == me:
+                    due[w[2]] = due.get(w[2], 0) + len(w[1])
+    left = sum(len(w[1]) for name, call in calls.items() for w in call if (name in HELPED) == (me >= N))
     V, A, P, Y = g.vector, g.scalar, g.tensor, g.sync
     COPY = ActivationFunctionType.Copy
     OP = AluOpType
@@ -134,6 +141,13 @@ def rank_program(g, core, T, topo):
             out.append(RemoteDMATransfer(dst_ids=[DstId(rid=rid, pnc=pid)], dma_engine_mask=sum(1 << e for e in eng),
                                          remote_sem=S[sem], src=view(T[buf], here, n), dst=view(T[buf], there, n)))
         g.remote_dma_fused(out, local_sem=S.left)
+
+    if me >= N:
+        for name, sem in zip(HELPED, ("r_az", "r_ac")):
+            g.wait_ge(S[sem], due[sem])
+            send(name)
+        g.wait_ge(S.left, left)
+        return
 
     def copy(q, o, i, sem):
         (q.activation(o, i, COPY) if q is A else q.tensor_copy(o, i)).then_inc(sem, 1)
@@ -196,8 +210,11 @@ def rank_program(g, core, T, topo):
     V.wait_ge(S.v_ga, 2)
     V.wait_ge(S.s_ga, 2)
     tiles = a_tiles(rank, side, nb)
-    for (inha, inac), sem in zip(tiles, (S.v_qa, S.v_qo)):
+
+    def quantise_a(inha, inac, sem):
         V.quantize_mx(T.ac[:, inac:inac + 128], T.az[:, inac:inac + 128], T.ha[:, 4 * inha:4 * inha + 512]).then_inc(sem, 1)
+
+    quantise_a(*tiles[0], S.v_qa)
 
     def ki(x):
         return T.ki[:, 16 * x:16 * x + 16]
@@ -226,6 +243,8 @@ def rank_program(g, core, T, topo):
     gather(A, 2, (0, 1, 2))
     gather(V, 1, (2, 3))
     quantise(1, HALF1, 2)
+    if len(tiles) == 2:
+        quantise_a(*tiles[1], S.v_qo)
     V.wait_ge(S.g_c, 5)
     V.wait_ge(S.d_p, 64)
     step(lambda: V.tensor_copy(T.lq[part(1), :], T.lq[part(0), :]))
@@ -236,8 +255,9 @@ def rank_program(g, core, T, topo):
          scalar(ki(1), picked, float(CI * lead), float(NA), OP.is_lt, OP.mult),
          scalar(kj(0), lj, -2.0, T.quarter[:, 0:1], OP.mult, OP.add))
     quantise(2, btile, 1)
+    step(scalar(kj(6), lj, 128.0, None, OP.add))
     step(add(ki(2), ki(0), ki(1)),
-         scalar(kj(1), lj, 256 + 31, None, OP.bitwise_and),
+         scalar(kj(1), kj(6), 256 + 31, None, OP.bitwise_and),
          scalar(kj(2), lj, 2, 32, OP.logical_shift_right, OP.bitwise_and),
          scalar(kj(3), kj(0), 192, None, OP.bitwise_and))
     step(add(kj(4), kj(1), kj(2)))
@@ -250,16 +270,18 @@ def rank_program(g, core, T, topo):
     send("a codes")
     send("a scales")
     g.wait_ge(S.v_q1, 1)
-    send("mate codes")
-    send("first scales")
+    send("help scales")
+    send("help codes")
+    send("far codes")
+    send("far scales")
     g.wait_ge(S.v_q2, 1)
     send("plane codes")
     send("second scales")
-    send("far codes")
     if len(tiles) == 2:
         g.wait_ge(S.v_qo, 1)
-    g.wait_ge(S.r_ad, due["r_ad"])
+    g.wait_ge(S.r_ac, due["r_ac"])
     send("on codes")
+    g.wait_ge(S.r_az, due["r_az"])
     send("on scales")
     g.wait_ge(S.left, left)
 
@@ -267,26 +289,32 @@ def rank_program(g, core, T, topo):
     P.wait_ge(S.v_q2, 1)
     if len(tiles) == 2:
         P.wait_ge(S.v_qo, 1)
-    for sem in ("r_ad", "r_ar"):
-        P.wait_ge(S[sem], due[sem])
-    for x, c in enumerate(order):
-        at = bown if x == 0 else CHUNKS + 128 * c
-        P.wait_ge(S["r_b%d" % c], due["r_b%d" % c])
-        P.matmul_mx(T.ps[:, 512 * x:512 * x + NA], T.bc[:, at:at + 128], T.bz[:, at:at + 128],
-                    T.ac[:, afirst:afirst + NA], T.az[:, afirst:afirst + NA], True, True).then_inc(S["m%d" % x], 1)
+    half = NA // 2
+    direct, handed = ((0, -32), (half, half - 32)) if rank == lead else ((half, half), (0, 0))
+    products = [(x, at, half, start) for at, start in (direct, handed) for x in (0, 1)] + [(2, 0, NA, 0), (3, 0, NA, 0)]
+    for y, (x, at, n, start) in enumerate(products):
+        c = order[x]
+        bat = bown if c == rank // 2 else CHUNKS + 128 * c
+        for sem in {0: ["r_ac", "r_az"], 2: ["r_ar"]}.get(y, []) + ["r_b%d" % c]:
+            P.wait_ge(S[sem], due[sem])
+        a, wd = afirst + start, max(n, 128)
+        P.matmul_mx(T.ps[:, 512 * y:512 * y + wd], T.bc[:, bat:bat + 128], T.bz[:, bat:bat + 128],
+                    T.ac[:, a:a + wd], T.az[:, a:a + wd], True, True).then_inc(S["m%d" % y], 1)
 
     for q in (V, A):
         q.wait_ge(S.v_oi, 1)
+    moves = []
     for n in range(2):
         z, t, u = T["z%d" % n], T["t%d" % n], T["u%d" % n]
         cp, vg, sg, vt = [S["%s%d" % (s, n)] for s in ("cp", "vg", "sg", "vt")]
-        col = 256 * (order[2 * n] // 2)
-        for q, x in ((A, 2 * n), (V, 2 * n + 1)):
-            at = NA * (order[x] % 2)
-            q.wait_ge(S["m%d" % x], 1)
-            copy(q, z[:, at:at + NA], T.ps[:, 512 * x:512 * x + NA], cp)
+        col = 256 * ((order[2 * n] + 1) // 2 % 2)
+        mine = [(y, p) for y, p in enumerate(products) if p[0] // 2 == n]
+        for y, (x, at, wd, start) in mine:
+            q, o, i = (A, V, A, A)[x], NA * (order[x] % 2) + at, 512 * y + at - start
+            q.wait_ge(S["m%d" % y], 1)
+            copy(q, z[:, o:o + wd], T.ps[:, i:i + wd], cp)
         for q, sem, hf in ((V, vg, 0), (A, sg, 1)):
-            q.wait_ge(cp, 2)
+            q.wait_ge(cp, len(mine))
             copy(q, t[:, 128 * hf:128 * hf + 128], z[:, :].indirect(T.oi[:, 8 * hf:8 * hf + 8]), sem)
 
         def turn(s, a, m):
@@ -300,16 +328,20 @@ def rank_program(g, core, T, topo):
         turn(2, 2, 2)
         for a in range(4):
             turn(3, a, 1)
+        moves.append((vt, u, col))
+    for vt, u, col in moves:
         A.wait_ge(vt, 1)
         for a in range(4):
             copy(A, T.rows[part((a + 1) % 4), col + 64:col + 128], u[part(a), :], S.s_f)
 
-    for q, sem, j in ((V, S.v_y, 0), (A, S.s_y, 12)):
+    for q, j in ((V, 0), (A, 6)):
         q.wait_ge(S.v_oj, 1)
         q.wait_ge(S.v_f, 14)
         q.wait_ge(S.s_f, 8)
-        copy(q, T.out[:, 16 * j:16 * j + 192], T.rows[:, 0:512].indirect(T.oj[:, j:j + 12]), sem)
-    for q, sem, done, j in ((Y, S.v_y, S.d_y0, 0), (A, S.s_y, S.d_y1, 192)):
-        q.wait_ge(sem, 1)
-        q.dma_start(T.y[:, j:j + 192], T.out[:, j:j + 192]).then_inc(done, 16)
-        q.wait_ge(done, 16)
+        for x in range(2):
+            o = j + 12 * x
+            copy(q, T.out[:, 16 * o:16 * o + 96], T.rows[:, 0:512].indirect(T.oj[:, o:o + 6]), S["y%d" % x])
+    for x, q in enumerate((Y, A)):
+        q.wait_ge(S["y%d" % x], 2)
+        q.dma_start(T.y[:, 192 * x:192 * x + 192], T.out[:, 192 * x:192 * x + 192]).then_inc(S["d_y%d" % x], 16)
+        q.wait_ge(S["d_y%d" % x], 16)

from concourse.bass import DstId, RemoteDMATransfer
from concourse.mybir import dt, AluOpType, ActivationFunctionType

N, CI, CJ, JW = 8, 24, 64, 384
NA = N * CI
CODES = "float8_e4m3fn_x4"
HALF1, CHUNKS = 192, 320
PAD, SPARE = 128 - CI, 304
HELPED = ("mate scales", "mate codes")

SCRATCH = {
    "aw": ("sbuf", [128, 1032], "bfloat16"), "bw": ("sbuf", [128, 1032], "bfloat16"),
    "ha": ("sbuf", [128, 1024], "bfloat16"), "h1": ("sbuf", [128, 512], "bfloat16"), "h2": ("sbuf", [128, 512], "bfloat16"),
    "ac": ("sbuf", [128, SPARE + 128], CODES), "az": ("sbuf", [128, SPARE + 128], "uint8"),
    "bc": ("sbuf", [128, 832], CODES), "bz": ("sbuf", [128, 832], "uint8"),
    "la": ("sbuf", [128, 3], "int32"), "lb": ("sbuf", [128, 16], "int32"), "lq": ("sbuf", [128, 32], "int32"),
    "oa": ("sbuf", [128, 16], "uint16"), "ob": ("sbuf", [128, 64], "uint16"),
    "oi": ("sbuf", [128, 16], "uint16"), "oj": ("sbuf", [128, 24], "uint16"), "oc": ("sbuf", [128, 2], "uint16"),
    "cq": ("sbuf", [128, 4], "int32"), "second": ("sbuf", [128, 16], "float32"), "quarter": ("sbuf", [128, 1], "float32"),
    "ki": ("sbuf", [128, 3 * 16], "float32"), "kj": ("sbuf", [128, 7 * 24], "int32"),
    "z0": ("sbuf", [128, 2 * NA], "float32"), "z1": ("sbuf", [128, 2 * NA], "float32"),
    "t0": ("sbuf", [128, 256], "float32"), "t1": ("sbuf", [128, 256], "float32"),
    "u0": ("sbuf", [128, 64], "float32"), "u1": ("sbuf", [128, 64], "float32"),
    "rows": ("sbuf", [128, 512], "float32"), "out": ("sbuf", [128, JW], "float32"),
    "ps": ("psum", [128, 3072], "float32"),
}
SEMAPHORES = (["d_a", "d_b", "d_sa", "d_sb", "d_p", "d_y0", "d_y1", "g_c",
               "v_z", "v_oa", "v_ob", "v_ga", "s_ga", "v_qa", "v_qo", "v_g1", "s_g1", "v_q1", "v_g2", "s_g2", "v_q2",
               "v_w", "v_oi", "v_oj", "v_f", "s_f", "y0", "y1", "left", "r_ac", "r_az", "r_ar"]
              + ["m%d" % n for n in range(6)] + ["r_b%d" % n for n in range(4)]
              + ["%s%d" % (s, n) for s in ("cp", "vg", "sg", "vt") for n in range(2)])


def places(T, topo):
    cores = list(T.cores)
    host0 = topo.host(cores[0])
    side = [0 if topo.host(c) == host0 else 1 for c in cores]
    gcol = [side[:r].count(side[r]) for r in range(N)]
    nb = [[q for q in range(N) if q != r and cores[q] in topo.cores_of(cores[r])][0] for r in range(N)]
    assert all(nb[r] // 2 == r // 2 for r in range(N))
    for c in cores[:N]:
        cores.append([h for h in topo.cores_of(c) if h not in cores and topo.die(h) == topo.die(c)
                      and all(topo.may_write(h, d) for d in cores[:N])][0])
    return cores, side, gcol, nb


def a_at(r, q, nb):
    return (PAD if r > nb[r] else 8) + CI * ((q - max(r, nb[r])) % N)


def a_run(r, nb):
    return [(r + x) % N for x in (range(4) if r > nb[r] else range(-3, 1))]


def a_tiles(r, side, nb):
    mine = PAD + CI * side[r]
    start = mine - PAD if r > nb[r] else mine
    tile = (start, a_at(r, r, nb) - (mine - start))
    return [tile] if start <= PAD and start + 128 >= PAD + 2 * CI else [(PAD, SPARE), tile]


def b_layout(r, gcol, nb):
    return (CJ, 0) if gcol[r] < gcol[nb[r]] else (0, CJ)


def b_at(r, q, gcol, nb):
    base = b_layout(r, gcol, nb)[1] if q // 2 == r // 2 else CHUNKS + 128 * (q // 2)
    return base + CJ * (1 - q % 2)


def plan(r, T, topo):
    cores, side, gcol, nb = places(T, topo)
    c, n = cores[r], nb[r]
    others = [q for q in range(N) if q not in (r, n)]
    off = topo.engines(c, cores[others[0]])
    near = [e for e in topo.engines(c, cores[n]) if e not in off]
    nc, nz = near, near
    h = len(off) // 2
    lo, hi, ev, od = off[:h], off[h:], off[0::2], off[1::2]
    mate = [q for q in others if side[q] == side[r]]
    plane = [q for q in others if topo.same_plane(c, cores[q])]
    far = [q for q in others if q not in mate + plane]
    inha, inac = a_tiles(r, side, nb)[0]

    def apiece(q, eng, buf):
        return (q, eng, "r_" + buf, buf, inac + PAD - inha + CI * side[q], a_at(q, r, nb), CI)

    def bpiece(q, eng, buf):
        here = b_layout(r, gcol, nb)[0] if gcol[q] // 2 == gcol[r] // 2 else HALF1
        return (q, eng, "r_b%d" % (r // 2), buf, here + CJ * (gcol[q] % 2), b_at(q, r, gcol, nb), CJ)

    af, ap, am = [[q for q in pair if r in a_run(q, nb)][0] for pair in (far, plane, mate)]
    head = a_run(r, nb)[0]
    return {
        "a codes": [apiece(af, lo, "ac"), apiece(ap, hi[:2], "ac"), apiece(am, hi[2:], "ac")],
        "a scales": [apiece(ap, hi, "az"), apiece(af, lo[:2], "az"), apiece(am, lo[2:], "az")],
        "help codes": [(N + r, nc, "r_ac", "bc", HALF1, HALF1, 2 * CJ)],
        "help scales": [(N + r, nz, "r_az", "bz", HALF1, HALF1, 2 * CJ)],
        "mate codes": [bpiece(mate[0], lo, "bc"), bpiece(mate[1], hi, "bc")],
        "mate scales": [bpiece(mate[0], lo, "bz"), bpiece(mate[1], hi, "bz")],
        "far codes": [bpiece(far[0], lo, "bc"), bpiece(far[1], hi, "bc")],
        "far scales": [bpiece(far[0], lo, "bz"), bpiece(far[1], hi, "bz")],
        "second scales": [bpiece(plane[0], lo, "bz"), bpiece(plane[1], hi, "bz"), bpiece(n, nz, "bz")],
        "plane codes": [bpiece(plane[0], lo, "bc"), bpiece(plane[1], hi, "bc"), bpiece(n, nc, "bc")],
        "on codes": [(n, near, "r_ar", "ac", a_at(r, head, nb), a_at(n, head, nb), 4 * CI)],
        "on scales": [(n, near, "r_ar", "az", a_at(r, head, nb), a_at(n, head, nb), 4 * CI)],
    }, [r // 2, far[0] // 2, plane[0] // 2, mate[0] // 2]


def view(t, a, n):
    v = t[:, a:a + n]
    return v.bitcast(dt.uint8) if t.dtype != dt.uint8 else v


def rank_program(g, core, T, topo):
    S = T.sem
    cores, side, gcol, nb = places(T, topo)
    if core not in cores:
        return
    me = cores.index(core)
    rank = me % N
    calls, order = plan(rank, T, topo)
    due = {}
    for q in range(N):
        for call in plan(q, T, topo)[0].values():
            for w in call:
                if w[0] == me:
                    due[w[2]] = due.get(w[2], 0) + len(w[1])
    left = sum(len(w[1]) for name, call in calls.items() for w in call if (name in HELPED) == (me >= N))
    V, A, P, Y = g.vector, g.scalar, g.tensor, g.sync
    COPY = ActivationFunctionType.Copy
    OP = AluOpType
    lead = max(rank, nb[rank])
    afirst = a_at(rank, lead, nb)
    btile, bown = b_layout(rank, gcol, nb)

    def send(name):
        out = []
        for q, eng, sem, buf, here, there, n in calls[name]:
            rid, pid = topo.addr(cores[q], core)
            out.append(RemoteDMATransfer(dst_ids=[DstId(rid=rid, pnc=pid)], dma_engine_mask=sum(1 << e for e in eng),
                                         remote_sem=S[sem], src=view(T[buf], here, n), dst=view(T[buf], there, n)))
        g.remote_dma_fused(out, local_sem=S.left)

    if me >= N:
        for name, sem in zip(HELPED, ("r_az", "r_ac")):
            g.wait_ge(S[sem], due[sem])
            send(name)
        g.wait_ge(S.left, left)
        return

    def copy(q, o, i, sem):
        (q.activation(o, i, COPY) if q is A else q.tensor_copy(o, i)).then_inc(sem, 1)

    def part(a, n=1):
        return slice(32 * a, 32 * (a + n))

    w = [0]

    def step(*insts):
        if w[0]:
            V.wait_ge(S.v_w, w[0])
        for inst in insts:
            inst().then_inc(S.v_w, 1)
        w[0] += len(insts)

    def scalar(o, i, *ops):
        return lambda: V.tensor_scalar(o, i, *ops)

    def add(o, i, j):
        return lambda: V.tensor_tensor(o, i, j, OP.add)

    for k in range(4, 8):
        A.dma_start(T.la[16 * k:16 * k + 16, :], T.sa[:, :]).then_inc(S.d_sa, 16)
    for k in range(4, 8):
        A.dma_start(T.lb[16 * k:16 * k + 16, :], T.sb[:, :]).then_inc(S.d_sb, 16)
    A.dma_start(T.bw[:, 8:1032], T.b[:, :]).then_inc(S.d_b, 16)
    for k in range(4):
        Y.dma_start(T.la[16 * k:16 * k + 16, :], T.sa[:, :]).then_inc(S.d_sa, 16)
    Y.dma_start(T.aw[:, 8:1032], T.a[:, :]).then_inc(S.d_a, 16)
    for k in range(4):
        Y.dma_start(T.lb[16 * k:16 * k + 16, :], T.sb[:, :]).then_inc(S.d_sb, 16)
    for k in range(2):
        Y.dma_start(T.lq[16 * k:16 * k + 16, 0:8], T.pi[:, :]).then_inc(S.d_p, 16)
        Y.dma_start(T.lq[16 * k:16 * k + 16, 8:32], T.pj[:, :]).then_inc(S.d_p, 16)

    for a in range(4):
        g.iota(T.cq[part(a), 0:1], [[0, 1]], 4 * a, 1).then_inc(S.g_c, 1)
    g.wait_ge(S.g_c, 4)
    g.iota(T.second[:, :], [[0, 4], [NA, 2], [0, 2]], -CI * lead, 0, allow_small_or_imprecise_dtypes=True).then_inc(S.g_c, 1)
    for z in (T.aw[:, 0:8], T.bw[:, 0:8], T.ha[:, 0:4 * PAD], T.ha[:, 4 * (PAD + 2 * CI):1024]):
        V.memset(z, 0.0).then_inc(S.v_z, 1)
    for b in range(4):
        V.memset(T.quarter[part(b), :], float(64 * b + 128 + 63 + 1024)).then_inc(S.v_z, 1)
    V.wait_ge(S.g_c, 4)
    step(scalar(T.cq[:, 1:2], T.cq[:, 0:1], 1, 6, OP.logical_shift_right, OP.bitwise_and),
         scalar(T.cq[:, 2:3], T.cq[:, 0:1], 1, None, OP.bitwise_and))
    step(add(T.cq[:, 3:4], T.cq[:, 1:2], T.cq[:, 2:3]))
    step(lambda: V.tensor_copy(T.oc[:, 0:1], T.cq[:, 3:4]))

    V.wait_ge(S.d_sa, 128)
    for t in range(4):
        V.tensor_scalar(T.oa[:, 4 * t:4 * t + 3], T.la[:, :], 4.0, float(8 + t), OP.mult, OP.add).then_inc(S.v_oa, 1)
    for q, sem in ((A, S.s_ga), (V, S.v_ga)):
        q.wait_ge(S.v_z, 8)
        q.wait_ge(S.v_oa, 4)
        q.wait_ge(S.d_a, 16)
        for t in ((0, 1) if q is A else (2, 3)):
            copy(q, T.ha[:, 4 * PAD + t:4 * (PAD + 2 * CI):4], T.aw[:, 0:1032].indirect(T.oa[:, 4 * t:4 * t + 3]), sem)
    V.wait_ge(S.v_ga, 2)
    V.wait_ge(S.s_ga, 2)
    tiles = a_tiles(rank, side, nb)

    def quantise_a(inha, inac, sem):
        V.quantize_mx(T.ac[:, inac:inac + 128], T.az[:, inac:inac + 128], T.ha[:, 4 * inha:4 * inha + 512]).then_inc(sem, 1)

    quantise_a(*tiles[0], S.v_qa)

    def ki(x):
        return T.ki[:, 16 * x:16 * x + 16]

    def kj(x):
        return T.kj[:, 24 * x:24 * x + 24]

    def gather(q, x, ts):
        pair = gcol[rank] // 2 if x == 2 else 1 - gcol[rank] // 2
        for t in ts:
            o = 16 * t + 8 * pair
            copy(q, T["h%d" % x][:, t:512:4], T.bw[:, 0:1032].indirect(T.ob[:, o:o + 8]), S["%s_g%d" % ("s" if q is A else "v", x)])

    def quantise(x, at, nv):
        V.wait_ge(S["v_g%d" % x], nv)
        V.wait_ge(S["s_g%d" % x], 4 - nv)
        V.quantize_mx(T.bc[:, at:at + 128], T.bz[:, at:at + 128], T["h%d" % x][:, :]).then_inc(S["v_q%d" % x], 1)

    V.wait_ge(S.d_sb, 128)
    for t in range(4):
        V.tensor_scalar(T.ob[:, 16 * t:16 * t + 16], T.lb[:, :], 4.0, float(8 + t), OP.mult, OP.add).then_inc(S.v_ob, 1)
    for q in (A, V):
        q.wait_ge(S.v_ob, 4)
        q.wait_ge(S.d_b, 16)
    gather(A, 1, (0, 1))
    gather(A, 2, (0, 1, 2))
    gather(V, 1, (2, 3))
    quantise(1, HALF1, 2)
    if len(tiles) == 2:
        quantise_a(*tiles[1], S.v_qo)
    V.wait_ge(S.g_c, 5)
    V.wait_ge(S.d_p, 64)
    step(lambda: V.tensor_copy(T.lq[part(1), :], T.lq[part(0), :]))
    gather(V, 2, (3,))
    step(lambda: V.tensor_copy(T.lq[part(2, 2), :], T.lq[part(0, 2), :]))
    picked, lj = T.lq[:, 0:8].indirect(T.oc[:, 0:1]), T.lq[:, 8:32]
    step(add(ki(0), picked, T.second[:, :]),
         scalar(ki(1), picked, float(CI * lead), float(NA), OP.is_lt, OP.mult),
         scalar(kj(0), lj, -2.0, T.quarter[:, 0:1], OP.mult, OP.add))
    quantise(2, btile, 1)
    step(scalar(kj(6), lj, 128.0, None, OP.add))
    step(add(ki(2), ki(0), ki(1)),
         scalar(kj(1), kj(6), 256 + 31, None, OP.bitwise_and),
         scalar(kj(2), lj, 2, 32, OP.logical_shift_right, OP.bitwise_and),
         scalar(kj(3), kj(0), 192, None, OP.bitwise_and))
    step(add(kj(4), kj(1), kj(2)))
    V.tensor_copy(T.oi[:, :], ki(2)).then_inc(S.v_oi, 1)
    step(add(kj(5), kj(4), kj(3)))
    step()
    V.tensor_copy(T.oj[:, :], kj(5)).then_inc(S.v_oj, 1)

    g.wait_ge(S.v_qa, 1)
    send("a codes")
    send("a scales")
    g.wait_ge(S.v_q1, 1)
    send("help scales")
    send("help codes")
    send("far codes")
    send("far scales")
    g.wait_ge(S.v_q2, 1)
    send("plane codes")
    send("second scales")
    if len(tiles) == 2:
        g.wait_ge(S.v_qo, 1)
    g.wait_ge(S.r_ac, due["r_ac"])
    send("on codes")
    g.wait_ge(S.r_az, due["r_az"])
    send("on scales")
    g.wait_ge(S.left, left)

    P.wait_ge(S.v_qa, 1)
    P.wait_ge(S.v_q2, 1)
    if len(tiles) == 2:
        P.wait_ge(S.v_qo, 1)
    half = NA // 2
    direct, handed = ((0, -32), (half, half - 32)) if rank == lead else ((half, half), (0, 0))
    products = [(x, at, half, start) for at, start in (direct, handed) for x in (0, 1)] + [(2, 0, NA, 0), (3, 0, NA, 0)]
    for y, (x, at, n, start) in enumerate(products):
        c = order[x]
        bat = bown if c == rank // 2 else CHUNKS + 128 * c
        for sem in {0: ["r_ac", "r_az"], 2: ["r_ar"]}.get(y, []) + ["r_b%d" % c]:
            P.wait_ge(S[sem], due[sem])
        a, wd = afirst + start, max(n, 128)
        P.matmul_mx(T.ps[:, 512 * y:512 * y + wd], T.bc[:, bat:bat + 128], T.bz[:, bat:bat + 128],
                    T.ac[:, a:a + wd], T.az[:, a:a + wd], True, True).then_inc(S["m%d" % y], 1)

    for q in (V, A):
        q.wait_ge(S.v_oi, 1)
    moves = []
    for n in range(2):
        z, t, u = T["z%d" % n], T["t%d" % n], T["u%d" % n]
        cp, vg, sg, vt = [S["%s%d" % (s, n)] for s in ("cp", "vg", "sg", "vt")]
        col = 256 * ((order[2 * n] + 1) // 2 % 2)
        mine = [(y, p) for y, p in enumerate(products) if p[0] // 2 == n]
        for y, (x, at, wd, start) in mine:
            q, o, i = (A, V, A, A)[x], NA * (order[x] % 2) + at, 512 * y + at - start
            q.wait_ge(S["m%d" % y], 1)
            copy(q, z[:, o:o + wd], T.ps[:, i:i + wd], cp)
        for q, sem, hf in ((V, vg, 0), (A, sg, 1)):
            q.wait_ge(cp, len(mine))
            copy(q, t[:, 128 * hf:128 * hf + 128], z[:, :].indirect(T.oi[:, 8 * hf:8 * hf + 8]), sem)

        def turn(s, a, m):
            V.transpose(T.rows[part((a + s) % 4, m), col + 64 * s:col + 64 * s + 64], t[part(a, m), 64 * s:64 * s + 64]).then_inc(S.v_f, 1)

        V.wait_ge(vg, 1)
        V.transpose(u[:, :], t[:, 64:128]).then_inc(vt, 1)
        turn(0, 0, 4)
        V.wait_ge(sg, 1)
        turn(2, 0, 2)
        turn(2, 2, 2)
        for a in range(4):
            turn(3, a, 1)
        moves.append((vt, u, col))
    for vt, u, col in moves:
        A.wait_ge(vt, 1)
        for a in range(4):
            copy(A, T.rows[part((a + 1) % 4), col + 64:col + 128], u[part(a), :], S.s_f)

    for q, j in ((V, 0), (A, 6)):
        q.wait_ge(S.v_oj, 1)
        q.wait_ge(S.v_f, 14)
        q.wait_ge(S.s_f, 8)
        for x in range(2):
            o = j + 12 * x
            copy(q, T.out[:, 16 * o:16 * o + 96], T.rows[:, 0:512].indirect(T.oj[:, o:o + 6]), S["y%d" % x])
    for x, q in enumerate((Y, A)):
        q.wait_ge(S["y%d" % x], 2)
        q.dma_start(T.y[:, 192 * x:192 * x + 192], T.out[:, 192 * x:192 * x + 192]).then_inc(S["d_y%d" % x], 16)
        q.wait_ge(S["d_y%d" % x], 16)
